import numpy as np
import ml_dtypes


def mxq(x, axis, fmt="e4m3"):
    dtype, down = {"e4m3": (ml_dtypes.float8_e4m3fn, 7), "e5m2": (ml_dtypes.float8_e5m2, 14)}[fmt]
    v = np.moveaxis(np.asarray(x, np.float32).astype(ml_dtypes.bfloat16).astype(np.float64), axis, -1)
    blocks = v.reshape(v.shape[:-1] + (-1, 32))
    amax = np.abs(blocks).max(-1, keepdims=True)
    byte = np.maximum(np.where(amax > 0, np.frexp(amax)[1] - 1 + 127, 0) - down, 1)
    scale = np.exp2(byte - 127.0)
    codes = (blocks / scale).astype(np.float32).astype(dtype).astype(np.float64)
    return np.moveaxis((codes * scale).reshape(v.shape), -1, axis)


WIDE = False


def mx_kscale(k):
    if not WIDE:
        return np.ones(k)
    levels = np.array([24, -24, 12, -12, 0])
    if k % 512:
        return np.exp2(np.random.permutation(np.resize(levels, k // 32))).repeat(32)
    a = np.empty((k // 512, 16))
    for p in range(k // 512):
        a[p, :8] = np.random.permutation(np.resize(levels, 8))
        for g in range(8):
            far = levels[np.abs(levels - a[p, g]) >= 10]
            a[p, g + 8] = far[np.random.randint(len(far))]
    return np.exp2(a.ravel()).repeat(32)


def f64(x):
    return np.asarray(x).astype(np.float64)


def striped(idx):
    return np.tile(idx.reshape(-1, 16).T, (8, 1)).astype(np.uint16)


def unstriped(offs):
    return offs[:16].T.reshape(-1).astype(np.int64)


E2M1 = np.array([0.0, 0.5, 1.0, 1.5, 2.0, 3.0, 4.0, 6.0, -0.0, -0.5, -1.0, -1.5, -2.0, -3.0, -4.0, -6.0])


def pack_weight(w, fmt):
    k, n = w.shape
    w = f64(np.asarray(w, np.float32).astype(ml_dtypes.bfloat16)).reshape(k // 32, 32, n)
    amax = np.abs(w).max(1)
    if fmt == "e4m3":
        byte = np.frexp(amax)[1] - 1 + 127 - 7
    else:
        mant, ex = np.frexp(amax / 6.0)
        byte = np.where(mant > 0.5, ex, ex - 1) + 127
    byte = np.clip(np.where(amax > 0, byte, 1), 1, 254)
    scaled = (w * np.exp2(127.0 - byte)[:, None, :]).reshape(k, n).astype(np.float32)
    by_word = np.ascontiguousarray(scaled.reshape(k // 512, 128, 4, n).transpose(0, 1, 3, 2))
    if fmt == "e4m3":
        words = by_word.astype(ml_dtypes.float8_e4m3fn).view(np.uint8)
    else:
        c = by_word.astype(ml_dtypes.float4_e2m1fn).view(np.uint8) & 0xF
        words = (c[..., 0::2] | (c[..., 1::2] << 4)).reshape(k // 512, 128, 2 * n)
    return np.ascontiguousarray(words), np.ascontiguousarray(byte.astype(np.uint8).reshape(k // 512, 16, n))


def unpack_weight(words, scales, fmt):
    g, _, n = scales.shape
    words = np.ascontiguousarray(words).reshape(g, 128, n, -1)
    if fmt == "e4m3":
        vals = words.view(ml_dtypes.float8_e4m3fn).astype(np.float64)
    else:
        nib = np.empty((g, 128, n, 4), np.uint8)
        nib[..., 0::2] = words & 0xF
        nib[..., 1::2] = words >> 4
        vals = E2M1[nib]
    vals = vals * np.repeat(np.exp2(scales.astype(np.float64) - 127.0), 8, axis=1)[..., None]
    return vals.transpose(0, 1, 3, 2).reshape(g * 512, n)


def split(x):
    m, e = np.frexp(f64(x))
    hi = np.ldexp(np.trunc(16.0 * m) / 16.0, e)
    return hi, f64(x) - hi


K, L, N, T, J = 512, 1024, 512, 2048, 512


def setup_inputs():
    n = np.random.standard_normal
    s = mx_kscale(K)[:, None]
    s2 = mx_kscale(L)[:, None]
    p_tab = pack_weight(n((K, T)) * s, "e4m3")
    return {
        "tab_words": p_tab[0],
        "tab_scales": p_tab[1],
        "w": (n((K, N)) / np.sqrt(K) / s).astype(np.float32),
        "x": (n((L, J)) * s2).astype(np.float32),
        "wx": (n((L, N)) / np.sqrt(L) / s2).astype(np.float32),
        "iw0": (np.random.uniform(0.1, 0.6, J)).astype(np.float32),
        "iw1": (np.random.uniform(0.1, 0.6, J)).astype(np.float32),
        "iw2": (np.random.uniform(0.1, 0.6, J)).astype(np.float32),
        "offs": striped(np.concatenate([np.random.permutation(T)[:J] for _ in range(3)])),
    }


def reference(tab_words, tab_scales, w, x, wx, iw0, iw1, iw2, offs):
    idx = unstriped(offs).reshape(3, J)
    tab_ = unpack_weight(tab_words, tab_scales, "e4m3")[:, idx]
    w_ = mxq(f64(w), 0, "e4m3")
    a0 = w_.T @ tab_[:, 0]
    a1 = w_.T @ tab_[:, 1]
    a2 = w_.T @ tab_[:, 2]
    x_ = mxq(f64(x), 0, "e4m3")
    wx_hi, wx_lo = split(wx)
    wx_hi_, wx_lo_ = mxq(wx_hi, 0, "e4m3"), mxq(wx_lo, 0, "e4m3")
    ax = wx_hi_.T @ x_ + wx_lo_.T @ x_
    return np.maximum(a0 * f64(iw0)[None, :] + a1 * f64(iw1)[None, :] + a2 * f64(iw2)[None, :] + ax, 0.0)

@@ -1,0 +1,296 @@
+from contextlib import ExitStack
+
+import concourse.mybir as mybir
+from concourse.masks import make_identity
+
+K, L, N, T, J, G = 512, 1024, 512, 2048, 512, 3
+FLOPS = 2 * N * J * (G * K + 2 * L)
+
+F32 = mybir.dt.float32
+BF16 = mybir.dt.bfloat16
+I32 = mybir.dt.int32
+U32 = mybir.dt.uint32
+U16 = mybir.dt.uint16
+U8 = mybir.dt.uint8
+FP8X4 = mybir.dt.float8_e4m3fn_x4
+ALU = mybir.AluOpType
+ACT = mybir.ActivationFunctionType
+
+P = 128
+PACK = 4
+TILES = 4
+HI_MASK = 0xFFF0FFF0 - (1 << 32)
+
+
+def rows_view(raw_ap, run):
+    return raw_ap.rearrange("p t (c i) -> p c t i", i=run)
+
+
+def woven_view(woven_ap, run):
+    return woven_ap.rearrange("p (c i t) -> p c t i", i=run, t=PACK)
+
+
+def tile_list_interp_hl_relu_kernel(
+    tc, tab_words, tab_scales, w, x, wx, iw0, iw1, iw2, offs, out
+):
+    nc = tc.nc
+    with ExitStack() as ctx:
+        sb = ctx.enter_context(tc.tile_pool(name="sb", bufs=1))
+        mx_psum = ctx.enter_context(tc.psum_pool(name="mx_psum", bufs=2))
+        out_psum = ctx.enter_context(tc.psum_pool(name="out_psum", bufs=1))
+
+        def sbuf(name, width, dtype):
+            return sb.tile([P, width], dtype, name=name, align_bytes=64)
+
+        def load_pass(name, src, a, c0, c1):
+            raw = sbuf(name, PACK * (c1 - c0), F32)
+            view = raw[:].rearrange("p (t c) -> p t c", t=PACK)
+            nc.sync.dma_start(
+                out=view,
+                in_=src[a * 512 : (a + 1) * 512, c0:c1].rearrange("(p t) c -> p t c", t=PACK),
+            )
+            return raw
+
+        def quantize(name, woven, codes, scales):
+            nc.vector.quantize_mx(out=codes.bitcast(FP8X4), scales=scales, in_=woven)
+
+        offsets = sb.tile([P, G * J // 16], U16, name="offsets")
+        table_scales = sbuf("table_scales", T, U8)
+        nc.vector.memset(table_scales[:].bitcast(I32), 0)
+        nc.sync.dma_start(offsets[:], offs)
+        for q in range(4):
+            nc.scalar.dma_start(
+                out=table_scales[32 * q : 32 * q + 4, :].bitcast(I32),
+                in_=tab_scales[0, 4 * q : 4 * q + 4, :].bitcast(I32),
+            )
+        w_raw = [load_pass("w_raw%d" % h, w, 0, 256 * h, 256 * (h + 1)) for h in range(2)]
+        table_words = sbuf("table_words", T, U32)
+        nc.sync.dma_start(
+            out=table_words[:].bitcast(I32),
+            in_=tab_words[0].rearrange("p t i -> p (t i)").bitcast(I32),
+        )
+        iw_rows = sbuf("iw_rows", P, F32)
+        nc.gpsimd.memset(iw_rows[:], 0.0)
+        ident = sbuf("ident", P, F32)
+        make_identity(nc, ident[:])
+        for g, iw in enumerate((iw0, iw1, iw2)):
+            nc.sync.dma_start(
+                out=iw_rows[TILES * g : TILES * (g + 1), :], in_=iw.rearrange("(c p) -> c p", p=P)
+            )
+        x_raw = [None, None]
+        wx_raw = [None, None]
+        wx_raw[0] = load_pass("wx_raw0", wx, 0, 0, N)
+        x_raw[0] = load_pass("x_raw0", x, 0, 0, J)
+        x_raw[1] = load_pass("x_raw1", x, 1, 0, J)
+        wx_raw[1] = load_pass("wx_raw1", wx, 1, 0, N)
+
+        def list_row(g):
+            return offsets[:, g * (J // 16) : (g + 1) * (J // 16)]
+
+        picked_scales = [sbuf("picked_scales%d" % g, J, U8) for g in range(G)]
+        picked_words = [sbuf("picked_words%d" % g, J, U32) for g in range(G)]
+        for g in range(G):
+            nc.vector.tensor_copy(picked_scales[g][:], table_scales[:].indirect(list_row(g)))
+
+        w_codes = sbuf("w_codes", N, U32)
+        w_scales = sbuf("w_scales", N, U8)
+        for h in range(2):
+            woven = sbuf("w_woven%d" % h, PACK * 256, BF16)
+            nc.scalar.activation(
+                woven_view(woven[:], 4),
+                rows_view(w_raw[h][:].rearrange("p (t c) -> p t c", t=PACK), 4),
+                ACT.Copy,
+            )
+            cols = slice(256 * h, 256 * (h + 1))
+            quantize("w", woven[:], w_codes[:, cols], w_scales[:, cols])
+
+        iw_bank = mx_psum.tile([P, N], F32, name="mx_bank")
+        nc.tensor.transpose(iw_bank[:, 0:P], iw_rows[:], ident[:])
+        iw_cols = sbuf("iw_cols", G * TILES, F32)
+        nc.scalar.activation(iw_cols[:], iw_bank[:, 0 : G * TILES], ACT.Copy)
+
+        for g in range(G):
+            nc.vector.tensor_copy(picked_words[g][:], table_words[:].indirect(list_row(g)))
+
+        out_banks = [out_psum.tile([P, J], F32, name="out_bank%d" % nt) for nt in range(TILES)]
+
+        def add_transposed(nt, jt, src, first, last):
+            nc.tensor.matmul(
+                out_banks[nt][:, jt * P : (jt + 1) * P], src, ident[:],
+                is_transpose=True, start=first, stop=last,
+            )
+
+        def project(g):
+            scaled = []
+            for jt in range(TILES):
+                cols = slice(jt * P, (jt + 1) * P)
+                bank = mx_psum.tile([P, N], F32, name="mx_bank")
+                nc.tensor.matmul_mx(
+                    out=bank[:],
+                    lhsT=picked_words[g][:, cols].bitcast(FP8X4),
+                    lhsT_scale=picked_scales[g][:, cols],
+                    rhs=w_codes[:].bitcast(FP8X4),
+                    rhs_scale=w_scales[:],
+                    start=True,
+                    stop=True,
+                )
+                s = sbuf("scaled%d_%d" % (g, jt), N, F32)
+                nc.scalar.activation(
+                    s[:], bank[:], ACT.Copy, scale=iw_cols[:, TILES * g + jt : TILES * g + jt + 1]
+                )
+                scaled.append(s)
+            return scaled
+
+        def turn(g, scaled):
+            for jt in range(TILES):
+                for nt in range(TILES):
+                    add_transposed(
+                        nt, jt, scaled[jt][:, nt * P : (nt + 1) * P], g == 0 and jt == 0,
+                        nt == TILES - 1 and g == G - 1 and jt == TILES - 1,
+                    )
+
+        x_codes = [sbuf("x_codes%d" % a, J, U32) for a in range(2)]
+        x_scales = [sbuf("x_scales%d" % a, J, U8) for a in range(2)]
+        x_woven = [sbuf("x_woven%d" % a, PACK * J, BF16) for a in range(2)]
+
+        def cast_x(a, c0, c1, on_vector):
+            dst = woven_view(x_woven[a][:, PACK * c0 : PACK * c1], 4)
+            src = rows_view(x_raw[a][:].rearrange("p (t c) -> p t c", t=PACK)[:, :, c0:c1], 4)
+            if on_vector:
+                nc.vector.tensor_copy(dst, src)
+            else:
+                nc.scalar.activation(dst, src, ACT.Copy)
+
+        def quantize_x(a):
+            quantize("x", x_woven[a][:], x_codes[a][:], x_scales[a][:])
+
+        def split_units(a, width):
+            units = []
+            raw = wx_raw[a]
+            halves = raw[:].bitcast(BF16).rearrange("p (t c h) -> p t c h", t=PACK, h=2)
+            rows = raw[:].rearrange("p (t c) -> p t c", t=PACK)
+            count = N // width
+            parts = [sbuf("parts%d_%d" % (a, u), 2 * PACK * width, BF16) for u in range(count)]
+            codes = [sbuf("wx_codes%d_%d" % (a, u), 2 * width, U32) for u in range(count)]
+            scales = [sbuf("wx_scales%d_%d" % (a, u), 2 * width, U8) for u in range(count)]
+
+            def trunc(u):
+                nc.vector.tensor_copy(
+                    woven_view(parts[u][:, 0 : PACK * width], 4),
+                    rows_view(halves[:, :, u * width : (u + 1) * width, 1], 4),
+                )
+
+            def mask(u):
+                hi_words = parts[u][:, 0 : PACK * width].bitcast(I32)
+                nc.vector.tensor_scalar(hi_words, hi_words, HI_MASK, None, ALU.bitwise_and)
+
+            def low(u):
+                nc.vector.tensor_tensor(
+                    woven_view(parts[u][:, PACK * width :], 2),
+                    rows_view(rows[:, :, u * width : (u + 1) * width], 2),
+                    woven_view(parts[u][:, 0 : PACK * width], 2),
+                    ALU.subtract,
+                )
+
+            def quant(u, first=0, last=2):
+                quantize(
+                    "wx",
+                    parts[u][:, PACK * width * first : PACK * width * last],
+                    codes[u][:, width * first : width * last],
+                    scales[u][:, width * first : width * last],
+                )
+
+            return trunc, mask, low, quant, codes, scales
+
+        s0 = project(0)
+        s1 = project(1)
+        turn(0, s0)
+        cast_x(0, 0, J, False)
+        turn(1, s1)
+        cast_x(1, 0, J // 2, False)
+        s2 = project(2)
+        turn(2, s2)
+        last_nt = TILES - 1
+        interpolated = sbuf("interpolated", J, F32)
+        nc.scalar.activation(interpolated[:], out_banks[last_nt][:], ACT.Copy)
+
+        trunc, mask, low, quant, codes0, scales0 = split_units(0, 256)
+        for step in (trunc, mask, low, quant):
+            for u in range(2):
+                step(u)
+        quantize_x(0)
+        cast_x(1, J // 2, J, True)
+
+        ax_banks = [
+            mx_psum.tile([P, N], F32, name="ax_bank" if nt < 2 else "mx_bank") for nt in range(TILES)
+        ]
+
+        def skip_passes(nt, a, codes, scales, width, parts=(0, 1)):
+            u, c0 = divmod(nt * P, width)
+            for part in parts:
+                ncols = slice(part * width + c0, part * width + c0 + P)
+                if nt == last_nt:
+                    nc.tensor.matmul_mx(
+                        out=ax_banks[nt][:],
+                        lhsT=codes[u][:, ncols].bitcast(FP8X4),
+                        lhsT_scale=scales[u][:, ncols],
+                        rhs=x_codes[a][:].bitcast(FP8X4),
+                        rhs_scale=x_scales[a][:],
+                        start=(a == 0 and part == 0),
+                        stop=(a == 1 and part == 1),
+                    )
+                    continue
+                for jt in range(TILES):
+                    jcols = slice(jt * P, (jt + 1) * P)
+                    nc.tensor.matmul_mx(
+                        out=ax_banks[nt][:, jcols],
+                        lhsT=x_codes[a][:, jcols].bitcast(FP8X4),
+                        lhsT_scale=x_scales[a][:, jcols],
+                        rhs=codes[u][:, ncols].bitcast(FP8X4),
+                        rhs_scale=scales[u][:, ncols],
+                        start=(a == 0 and part == 0 and jt == 0),
+                        stop=(a == 1 and part == 1 and jt == TILES - 1),
+                    )
+
+        for nt in range(TILES):
+            skip_passes(nt, 0, codes0, scales0, 256)
+
+        trunc, mask, low, quant, codes1, scales1 = split_units(1, P)
+
+        def finish(nt):
+            skip_passes(nt, 1, codes1, scales1, P)
+            result = sbuf("result%d" % nt, J, F32)
+            if nt == last_nt:
+                total = sbuf("total", J, F32)
+                nc.vector.tensor_tensor(total[:], ax_banks[nt][:], interpolated[:], ALU.add)
+                nc.vector.tensor_scalar(result[:], total[:], 0.0, None, ALU.max)
+            else:
+                ax = sbuf("ax%d" % nt, J, F32)
+                nc.scalar.activation(ax[:], ax_banks[nt][:], ACT.Copy)
+                for jt in range(TILES):
+                    add_transposed(nt, jt, ax[:, jt * P : (jt + 1) * P], False, jt == TILES - 1)
+                nc.scalar.activation(result[:], out_banks[nt][:], ACT.Relu)
+            nc.sync.dma_start(out=out[nt * P : (nt + 1) * P, :], in_=result[:])
+
+        trunc(0)
+        trunc(1)
+        mask(0)
+        quantize_x(1)
+        low(0)
+        mask(1)
+        quant(0)
+        finish(0)
+        low(1)
+        trunc(2)
+        quant(1)
+        finish(1)
+        mask(2)
+        trunc(3)
+        low(2)
+        mask(3)
+        quant(2)
+        finish(2)
+        low(3)
+        quant(3, 0, 1)
+        quant(3, 1, 2)
+        finish(3)

@@ -36,7 +36,7 @@ def tile_list_interp_hl_relu_kernel(
     nc = tc.nc
     with ExitStack() as ctx:
         sb = ctx.enter_context(tc.tile_pool(name="sb", bufs=1))
-        mx_psum = ctx.enter_context(tc.psum_pool(name="mx_psum", bufs=2))
+        mx_psum = ctx.enter_context(tc.psum_pool(name="mx_psum", bufs=1))
         out_psum = ctx.enter_context(tc.psum_pool(name="out_psum", bufs=1))
 
         def sbuf(name, width, dtype):
@@ -56,14 +56,16 @@ def tile_list_interp_hl_relu_kernel(
 
         offsets = sb.tile([P, G * J // 16], U16, name="offsets")
         table_scales = sbuf("table_scales", T, U8)
-        nc.vector.memset(table_scales[:].bitcast(I32), 0)
+        nc.vector.memset(table_scales[:, 0 : T // 2].bitcast(I32), 0)
+        nc.gpsimd.memset(table_scales[:, T // 2 :].bitcast(I32), 0)
         nc.sync.dma_start(offsets[:], offs)
         for q in range(4):
-            nc.scalar.dma_start(
+            nc.sync.dma_start(
                 out=table_scales[32 * q : 32 * q + 4, :].bitcast(I32),
                 in_=tab_scales[0, 4 * q : 4 * q + 4, :].bitcast(I32),
             )
-        w_raw = [load_pass("w_raw%d" % h, w, 0, 256 * h, 256 * (h + 1)) for h in range(2)]
+        w_cuts = (0, 128, N)
+        w_raw = [load_pass("w_raw%d" % h, w, 0, w_cuts[h], w_cuts[h + 1]) for h in range(2)]
         table_words = sbuf("table_words", T, U32)
         nc.sync.dma_start(
             out=table_words[:].bitcast(I32),
@@ -79,8 +81,9 @@ def tile_list_interp_hl_relu_kernel(
             )
         x_raw = [None, None]
         wx_raw = [None, None]
+        x0a = load_pass("x_raw0a", x, 0, 0, J // 2)
         wx_raw[0] = load_pass("wx_raw0", wx, 0, 0, N)
-        x_raw[0] = load_pass("x_raw0", x, 0, 0, J)
+        x0b = load_pass("x_raw0b", x, 0, J // 2, J)
         x_raw[1] = load_pass("x_raw1", x, 1, 0, J)
         wx_raw[1] = load_pass("wx_raw1", wx, 1, 0, N)
 
@@ -94,17 +97,16 @@ def tile_list_interp_hl_relu_kernel(
 
         w_codes = sbuf("w_codes", N, U32)
         w_scales = sbuf("w_scales", N, U8)
+        w_woven = sbuf("w_woven", PACK * N, BF16)
         for h in range(2):
-            woven = sbuf("w_woven%d" % h, PACK * 256, BF16)
             nc.scalar.activation(
-                woven_view(woven[:], 4),
+                woven_view(w_woven[:, PACK * w_cuts[h] : PACK * w_cuts[h + 1]], 4),
                 rows_view(w_raw[h][:].rearrange("p (t c) -> p t c", t=PACK), 4),
                 ACT.Copy,
             )
-            cols = slice(256 * h, 256 * (h + 1))
-            quantize("w", woven[:], w_codes[:, cols], w_scales[:, cols])
+        quantize("w", w_woven[:], w_codes[:], w_scales[:])
 
-        iw_bank = mx_psum.tile([P, N], F32, name="mx_bank")
+        iw_bank = mx_psum.tile([P, N], F32, name="mx_bank3")
         nc.tensor.transpose(iw_bank[:, 0:P], iw_rows[:], ident[:])
         iw_cols = sbuf("iw_cols", G * TILES, F32)
         nc.scalar.activation(iw_cols[:], iw_bank[:, 0 : G * TILES], ACT.Copy)
@@ -124,7 +126,7 @@ def tile_list_interp_hl_relu_kernel(
             scaled = []
             for jt in range(TILES):
                 cols = slice(jt * P, (jt + 1) * P)
-                bank = mx_psum.tile([P, N], F32, name="mx_bank")
+                bank = mx_psum.tile([P, N], F32, name="mx_bank%d" % (jt if g < G - 1 else 2 + jt % 2))
                 nc.tensor.matmul_mx(
                     out=bank[:],
                     lhsT=picked_words[g][:, cols].bitcast(FP8X4),
@@ -146,7 +148,7 @@ def tile_list_interp_hl_relu_kernel(
                 for nt in range(TILES):
                     add_transposed(
                         nt, jt, scaled[jt][:, nt * P : (nt + 1) * P], g == 0 and jt == 0,
-                        nt == TILES - 1 and g == G - 1 and jt == TILES - 1,
+                        nt in [2,3] and g == G - 1 and jt == TILES - 1,
                     )
 
         x_codes = [sbuf("x_codes%d" % a, J, U32) for a in range(2)]
@@ -155,7 +157,10 @@ def tile_list_interp_hl_relu_kernel(
 
         def cast_x(a, c0, c1, on_vector):
             dst = woven_view(x_woven[a][:, PACK * c0 : PACK * c1], 4)
-            src = rows_view(x_raw[a][:].rearrange("p (t c) -> p t c", t=PACK)[:, :, c0:c1], 4)
+            if a == 0:
+                src = rows_view((x0a if c0 == 0 else x0b)[:].rearrange("p (t c) -> p t c", t=PACK), 4)
+            else:
+                src = rows_view(x_raw[a][:].rearrange("p (t c) -> p t c", t=PACK)[:, :, c0:c1], 4)
             if on_vector:
                 nc.vector.tensor_copy(dst, src)
             else:
@@ -174,8 +179,8 @@ def tile_list_interp_hl_relu_kernel(
             codes = [sbuf("wx_codes%d_%d" % (a, u), 2 * width, U32) for u in range(count)]
             scales = [sbuf("wx_scales%d_%d" % (a, u), 2 * width, U8) for u in range(count)]
 
-            def trunc(u):
-                nc.vector.tensor_copy(
+            def trunc(u, on_scalar=False):
+                (nc.scalar.copy if on_scalar else nc.vector.tensor_copy)(
                     woven_view(parts[u][:, 0 : PACK * width], 4),
                     rows_view(halves[:, :, u * width : (u + 1) * width, 1], 4),
                 )
@@ -202,34 +207,32 @@ def tile_list_interp_hl_relu_kernel(
 
             return trunc, mask, low, quant, codes, scales
 
+        cast_x(0, 0, J // 2, False)
         s0 = project(0)
         s1 = project(1)
         turn(0, s0)
-        cast_x(0, 0, J, False)
         turn(1, s1)
-        cast_x(1, 0, J // 2, False)
+        cast_x(1, 0, J, False)
         s2 = project(2)
         turn(2, s2)
-        last_nt = TILES - 1
-        interpolated = sbuf("interpolated", J, F32)
-        nc.scalar.activation(interpolated[:], out_banks[last_nt][:], ACT.Copy)
-
         trunc, mask, low, quant, codes0, scales0 = split_units(0, 256)
         for step in (trunc, mask, low, quant):
-            for u in range(2):
-                step(u)
+            step(0)
+        cast_x(0, J // 2, J, True)
         quantize_x(0)
-        cast_x(1, J // 2, J, True)
+        for step in (trunc, mask, low, quant):
+            step(1)
+        direct = [2,3]
 
         ax_banks = [
-            mx_psum.tile([P, N], F32, name="ax_bank" if nt < 2 else "mx_bank") for nt in range(TILES)
+            mx_psum.tile([P, N], F32, name="mx_bank%d" % nt) for nt in range(TILES)
         ]
 
         def skip_passes(nt, a, codes, scales, width, parts=(0, 1)):
             u, c0 = divmod(nt * P, width)
             for part in parts:
                 ncols = slice(part * width + c0, part * width + c0 + P)
-                if nt == last_nt:
+                if nt in direct:
                     nc.tensor.matmul_mx(
                         out=ax_banks[nt][:],
                         lhsT=codes[u][:, ncols].bitcast(FP8X4),
@@ -252,18 +255,31 @@ def tile_list_interp_hl_relu_kernel(
                         stop=(a == 1 and part == 1 and jt == TILES - 1),
                     )
 
-        for nt in range(TILES):
-            skip_passes(nt, 0, codes0, scales0, 256)
-
         trunc, mask, low, quant, codes1, scales1 = split_units(1, P)
 
         def finish(nt):
             skip_passes(nt, 1, codes1, scales1, P)
             result = sbuf("result%d" % nt, J, F32)
-            if nt == last_nt:
-                total = sbuf("total", J, F32)
-                nc.vector.tensor_tensor(total[:], ax_banks[nt][:], interpolated[:], ALU.add)
-                nc.vector.tensor_scalar(result[:], total[:], 0.0, None, ALU.max)
+            if nt in direct:
+                if nt == TILES - 1:
+                    for h in range(2):
+                        cols = slice(h * 256, (h + 1) * 256)
+                        tot = sbuf("tot%d" % h, 256, F32)
+                        res = sbuf("res%d" % h, 256, F32)
+                        nc.vector.tensor_tensor(tot[:], ax_banks[nt][:, cols], interpolated[nt][:, cols], ALU.add)
+                        if h == 0:
+                            nc.scalar.activation(res[:], tot[:], ACT.Relu)
+                            nc.scalar.dma_start(out=out[nt * P : (nt + 1) * P, cols], in_=res[:])
+                        else:
+                            nc.vector.tensor_scalar(res[:], tot[:], 0.0, None, ALU.max)
+                            nc.sync.dma_start(out=out[nt * P : (nt + 1) * P, cols], in_=res[:])
+                    return
+                total = sbuf("total%d" % nt, J, F32)
+                nc.vector.tensor_tensor(total[:], ax_banks[nt][:], interpolated[nt][:], ALU.add)
+                if nt in [3]:
+                    nc.vector.tensor_scalar(result[:], total[:], 0.0, None, ALU.max)
+                else:
+                    nc.scalar.activation(result[:], total[:], ACT.Relu)
             else:
                 ax = sbuf("ax%d" % nt, J, F32)
                 nc.scalar.activation(ax[:], ax_banks[nt][:], ACT.Copy)
@@ -272,25 +288,33 @@ def tile_list_interp_hl_relu_kernel(
                 nc.scalar.activation(result[:], out_banks[nt][:], ACT.Relu)
             nc.sync.dma_start(out=out[nt * P : (nt + 1) * P, :], in_=result[:])
 
-        trunc(0)
-        trunc(1)
-        mask(0)
+        skip_passes(0, 0, codes0, scales0, 256)
+        skip_passes(1, 0, codes0, scales0, 256)
         quantize_x(1)
+        trunc(0)
+        trunc(1, True)
+        mask(0)
         low(0)
         mask(1)
         quant(0)
+        trunc(2, True)
+        trunc(3, True)
         finish(0)
+        skip_passes(2, 0, codes0, scales0, 256)
+        skip_passes(3, 0, codes0, scales0, 256)
         low(1)
-        trunc(2)
+        mask(2)
         quant(1)
         finish(1)
-        mask(2)
-        trunc(3)
+        interpolated = {}
+        for nt in direct:
+            interpolated[nt] = sbuf("interpolated%d" % nt, J, F32)
+            nc.scalar.activation(interpolated[nt][:], out_banks[nt][:], ACT.Copy)
         low(2)
         mask(3)
         quant(2)
-        finish(2)
-        low(3)
         quant(3, 0, 1)
+        low(3)
         quant(3, 1, 2)
+        finish(2)
         finish(3)

@@ -18,16 +18,29 @@ ACT = mybir.ActivationFunctionType
 
 P = 128
 PACK = 4
-TILES = 4
+K_PASS = P * PACK
+TILES = N // P
+HALF = J // 2
+LIST_COLS = J // 16
 HI_MASK = 0xFFF0FFF0 - (1 << 32)
+W_HEAD = 256
+COPY_RUN = 4
+SUB_RUN = 2
+TURNED_TILES = 2
+LAST_BANKS = 2
+SCALAR_TRUNCATES = (2, 3)
 
 
-def rows_view(raw_ap, run):
-    return raw_ap.rearrange("p t (c i) -> p c t i", i=run)
+def by_rows(raw):
+    return raw.rearrange("p (t c) -> p t c", t=PACK)
 
 
-def woven_view(woven_ap, run):
-    return woven_ap.rearrange("p (c i t) -> p c t i", i=run, t=PACK)
+def read_order(rows, run):
+    return rows.rearrange("p t (c i) -> p c t i", i=run)
+
+
+def write_order(woven, run):
+    return woven.rearrange("p (c i t) -> p c t i", i=run, t=PACK)
 
 
 def tile_list_interp_hl_relu_kernel(
@@ -36,285 +49,254 @@ def tile_list_interp_hl_relu_kernel(
     nc = tc.nc
     with ExitStack() as ctx:
         sb = ctx.enter_context(tc.tile_pool(name="sb", bufs=1))
-        mx_psum = ctx.enter_context(tc.psum_pool(name="mx_psum", bufs=1))
-        out_psum = ctx.enter_context(tc.psum_pool(name="out_psum", bufs=1))
+        psum = ctx.enter_context(tc.psum_pool(name="psum", bufs=1))
 
-        def sbuf(name, width, dtype):
-            return sb.tile([P, width], dtype, name=name, align_bytes=64)
+        def sbuf(name, width, dtype, slot=None):
+            return sb.tile([P, width], dtype, name=name, tag=slot or name, align_bytes=64)
 
-        def load_pass(name, src, a, c0, c1):
+        def mx_bank(b):
+            return psum.tile([P, N], F32, name="mx_bank%d" % b)
+
+        def load_rows(name, src, a, c0, c1):
             raw = sbuf(name, PACK * (c1 - c0), F32)
-            view = raw[:].rearrange("p (t c) -> p t c", t=PACK)
             nc.sync.dma_start(
-                out=view,
-                in_=src[a * 512 : (a + 1) * 512, c0:c1].rearrange("(p t) c -> p t c", t=PACK),
+                out=by_rows(raw[:]),
+                in_=src[a * K_PASS : (a + 1) * K_PASS, c0:c1].rearrange("(p t) c -> p t c", t=PACK),
             )
             return raw
 
-        def quantize(name, woven, codes, scales):
+        def weave(woven, raw, on_vector):
+            dst, src = write_order(woven, COPY_RUN), read_order(by_rows(raw[:]), COPY_RUN)
+            if on_vector:
+                nc.vector.tensor_copy(dst, src)
+            else:
+                nc.scalar.activation(dst, src, ACT.Copy)
+
+        def quantize(woven, codes, scales):
             nc.vector.quantize_mx(out=codes.bitcast(FP8X4), scales=scales, in_=woven)
 
-        offsets = sb.tile([P, G * J // 16], U16, name="offsets")
+        def mx_pass(bank, lhs, lhs_cols, rhs, rhs_cols, start, stop):
+            nc.tensor.matmul_mx(
+                out=bank,
+                lhsT=lhs[0][:, lhs_cols].bitcast(FP8X4),
+                lhsT_scale=lhs[1][:, lhs_cols],
+                rhs=rhs[0][:, rhs_cols].bitcast(FP8X4),
+                rhs_scale=rhs[1][:, rhs_cols],
+                start=start,
+                stop=stop,
+            )
+
+        offsets = sb.tile([P, G * LIST_COLS], U16, name="offsets")
         table_scales = sbuf("table_scales", T, U8)
         nc.vector.memset(table_scales[:, 0 : T // 2].bitcast(I32), 0)
         nc.gpsimd.memset(table_scales[:, T // 2 :].bitcast(I32), 0)
+        iw_rows = sbuf("iw_rows", P, F32)
+        nc.gpsimd.memset(iw_rows[:], 0.0)
+        ident = sbuf("ident", P, F32)
+        make_identity(nc, ident[:])
+
+        w_raw_head = load_rows("w_raw_head", w, 0, 0, W_HEAD)
         nc.sync.dma_start(offsets[:], offs)
         for q in range(4):
             nc.sync.dma_start(
                 out=table_scales[32 * q : 32 * q + 4, :].bitcast(I32),
                 in_=tab_scales[0, 4 * q : 4 * q + 4, :].bitcast(I32),
             )
-        w_cuts = (0, 128, N)
-        w_raw = [load_pass("w_raw%d" % h, w, 0, w_cuts[h], w_cuts[h + 1]) for h in range(2)]
+        w_raw_rest = load_rows("w_raw_rest", w, 0, W_HEAD, N)
         table_words = sbuf("table_words", T, U32)
         nc.sync.dma_start(
             out=table_words[:].bitcast(I32),
             in_=tab_words[0].rearrange("p t i -> p (t i)").bitcast(I32),
         )
-        iw_rows = sbuf("iw_rows", P, F32)
-        nc.gpsimd.memset(iw_rows[:], 0.0)
-        ident = sbuf("ident", P, F32)
-        make_identity(nc, ident[:])
         for g, iw in enumerate((iw0, iw1, iw2)):
             nc.sync.dma_start(
                 out=iw_rows[TILES * g : TILES * (g + 1), :], in_=iw.rearrange("(c p) -> c p", p=P)
             )
-        x_raw = [None, None]
-        wx_raw = [None, None]
-        x0a = load_pass("x_raw0a", x, 0, 0, J // 2)
-        wx_raw[0] = load_pass("wx_raw0", wx, 0, 0, N)
-        x0b = load_pass("x_raw0b", x, 0, J // 2, J)
-        x_raw[1] = load_pass("x_raw1", x, 1, 0, J)
-        wx_raw[1] = load_pass("wx_raw1", wx, 1, 0, N)
+        x0_raw_left = load_rows("x0_raw_left", x, 0, 0, HALF)
+        wx0_raw = load_rows("wx0_raw", wx, 0, 0, N)
+        x0_raw_right = load_rows("x0_raw_right", x, 0, HALF, J)
+        x1_raw = load_rows("x1_raw", x, 1, 0, J)
+        wx1_raw = load_rows("wx1_raw", wx, 1, 0, N)
 
-        def list_row(g):
-            return offsets[:, g * (J // 16) : (g + 1) * (J // 16)]
+        picked_scales = sbuf("picked_scales", G * J, U8)
+        nc.vector.tensor_copy(picked_scales[:], table_scales[:].indirect(offsets[:]))
 
-        picked_scales = [sbuf("picked_scales%d" % g, J, U8) for g in range(G)]
-        picked_words = [sbuf("picked_words%d" % g, J, U32) for g in range(G)]
-        for g in range(G):
-            nc.vector.tensor_copy(picked_scales[g][:], table_scales[:].indirect(list_row(g)))
-
-        w_codes = sbuf("w_codes", N, U32)
-        w_scales = sbuf("w_scales", N, U8)
         w_woven = sbuf("w_woven", PACK * N, BF16)
-        for h in range(2):
-            nc.scalar.activation(
-                woven_view(w_woven[:, PACK * w_cuts[h] : PACK * w_cuts[h + 1]], 4),
-                rows_view(w_raw[h][:].rearrange("p (t c) -> p t c", t=PACK), 4),
-                ACT.Copy,
-            )
-        quantize("w", w_woven[:], w_codes[:], w_scales[:])
+        weave(w_woven[:, 0 : PACK * W_HEAD], w_raw_head, False)
+        weave(w_woven[:, PACK * W_HEAD :], w_raw_rest, False)
+        w_mx = (sbuf("w_codes", N, U32), sbuf("w_scales", N, U8))
+        quantize(w_woven[:], w_mx[0][:], w_mx[1][:])
 
-        iw_bank = mx_psum.tile([P, N], F32, name="mx_bank3")
+        iw_bank = mx_bank(TILES - 1)
         nc.tensor.transpose(iw_bank[:, 0:P], iw_rows[:], ident[:])
         iw_cols = sbuf("iw_cols", G * TILES, F32)
         nc.scalar.activation(iw_cols[:], iw_bank[:, 0 : G * TILES], ACT.Copy)
 
-        for g in range(G):
-            nc.vector.tensor_copy(picked_words[g][:], table_words[:].indirect(list_row(g)))
+        picked_words = sbuf("picked_words", G * J, U32, slot="iw_rows")
+        for c0, c1 in ((0, HALF), (HALF, J), (J, 2 * J), (2 * J, 3 * J)):
+            nc.vector.tensor_copy(
+                picked_words[:, c0:c1], table_words[:].indirect(offsets[:, c0 // 16 : c1 // 16])
+            )
+        picked_mx = (picked_words, picked_scales)
 
-        out_banks = [out_psum.tile([P, J], F32, name="out_bank%d" % nt) for nt in range(TILES)]
+        out_banks = [psum.tile([P, J], F32, name="out_bank%d" % nt) for nt in range(TILES)]
 
-        def add_transposed(nt, jt, src, first, last):
+        def add_transposed(nt, jt, src, start, stop):
             nc.tensor.matmul(
                 out_banks[nt][:, jt * P : (jt + 1) * P], src, ident[:],
-                is_transpose=True, start=first, stop=last,
+                is_transpose=True, start=start, stop=stop,
             )
 
         def project(g):
-            scaled = []
+            scaled = sbuf("scaled%d" % g, TILES * N, F32, slot="x0_raw_left" if g == 0 else None)
             for jt in range(TILES):
-                cols = slice(jt * P, (jt + 1) * P)
-                bank = mx_psum.tile([P, N], F32, name="mx_bank%d" % (jt if g < G - 1 else 2 + jt % 2))
-                nc.tensor.matmul_mx(
-                    out=bank[:],
-                    lhsT=picked_words[g][:, cols].bitcast(FP8X4),
-                    lhsT_scale=picked_scales[g][:, cols],
-                    rhs=w_codes[:].bitcast(FP8X4),
-                    rhs_scale=w_scales[:],
-                    start=True,
-                    stop=True,
-                )
-                s = sbuf("scaled%d_%d" % (g, jt), N, F32)
+                bank = mx_bank(jt if g < G - 1 else TILES - LAST_BANKS + jt % LAST_BANKS)
+                places = slice(g * J + jt * P, g * J + (jt + 1) * P)
+                mx_pass(bank[:], picked_mx, places, w_mx, slice(0, N), True, True)
+                col = TILES * g + jt
                 nc.scalar.activation(
-                    s[:], bank[:], ACT.Copy, scale=iw_cols[:, TILES * g + jt : TILES * g + jt + 1]
+                    scaled[:, jt * N : (jt + 1) * N], bank[:], ACT.Copy, scale=iw_cols[:, col : col + 1]
                 )
-                scaled.append(s)
             return scaled
 
         def turn(g, scaled):
             for jt in range(TILES):
                 for nt in range(TILES):
-                    add_transposed(
-                        nt, jt, scaled[jt][:, nt * P : (nt + 1) * P], g == 0 and jt == 0,
-                        nt in [2,3] and g == G - 1 and jt == TILES - 1,
-                    )
+                    first = g == 0 and jt == 0
+                    last = g == G - 1 and jt == TILES - 1 and nt >= TURNED_TILES
+                    add_transposed(nt, jt, scaled[:, jt * N + nt * P : jt * N + (nt + 1) * P], first, last)
 
-        x_codes = [sbuf("x_codes%d" % a, J, U32) for a in range(2)]
-        x_scales = [sbuf("x_scales%d" % a, J, U8) for a in range(2)]
         x_woven = [sbuf("x_woven%d" % a, PACK * J, BF16) for a in range(2)]
-
-        def cast_x(a, c0, c1, on_vector):
-            dst = woven_view(x_woven[a][:, PACK * c0 : PACK * c1], 4)
-            if a == 0:
-                src = rows_view((x0a if c0 == 0 else x0b)[:].rearrange("p (t c) -> p t c", t=PACK), 4)
-            else:
-                src = rows_view(x_raw[a][:].rearrange("p (t c) -> p t c", t=PACK)[:, :, c0:c1], 4)
-            if on_vector:
-                nc.vector.tensor_copy(dst, src)
-            else:
-                nc.scalar.activation(dst, src, ACT.Copy)
+        x_mx = [(sbuf("x_codes%d" % a, J, U32), sbuf("x_scales%d" % a, J, U8)) for a in range(2)]
 
         def quantize_x(a):
-            quantize("x", x_woven[a][:], x_codes[a][:], x_scales[a][:])
+            quantize(x_woven[a][:], x_mx[a][0][:], x_mx[a][1][:])
 
-        def split_units(a, width):
-            units = []
-            raw = wx_raw[a]
-            halves = raw[:].bitcast(BF16).rearrange("p (t c h) -> p t c h", t=PACK, h=2)
-            rows = raw[:].rearrange("p (t c) -> p t c", t=PACK)
+        def split_steps(a, raw, width):
             count = N // width
             parts = [sbuf("parts%d_%d" % (a, u), 2 * PACK * width, BF16) for u in range(count)]
-            codes = [sbuf("wx_codes%d_%d" % (a, u), 2 * width, U32) for u in range(count)]
-            scales = [sbuf("wx_scales%d_%d" % (a, u), 2 * width, U8) for u in range(count)]
+            wx_mx = [
+                (sbuf("wx_codes%d_%d" % (a, u), 2 * width, U32), sbuf("wx_scales%d_%d" % (a, u), 2 * width, U8))
+                for u in range(count)
+            ]
+            upper_halves = raw[:].bitcast(BF16).rearrange("p (t c h) -> p t c h", t=PACK, h=2)
 
-            def trunc(u, on_scalar=False):
-                (nc.scalar.copy if on_scalar else nc.vector.tensor_copy)(
-                    woven_view(parts[u][:, 0 : PACK * width], 4),
-                    rows_view(halves[:, :, u * width : (u + 1) * width, 1], 4),
-                )
+            def truncate(u, on_scalar=False):
+                dst = write_order(parts[u][:, 0 : PACK * width], COPY_RUN)
+                src = read_order(upper_halves[:, :, u * width : (u + 1) * width, 1], COPY_RUN)
+                if on_scalar:
+                    nc.scalar.copy(dst, src)
+                else:
+                    nc.vector.tensor_copy(dst, src)
 
             def mask(u):
-                hi_words = parts[u][:, 0 : PACK * width].bitcast(I32)
-                nc.vector.tensor_scalar(hi_words, hi_words, HI_MASK, None, ALU.bitwise_and)
+                hi_pairs = parts[u][:, 0 : PACK * width].bitcast(I32)
+                nc.vector.tensor_scalar(hi_pairs, hi_pairs, HI_MASK, None, ALU.bitwise_and)
 
-            def low(u):
+            def subtract(u):
                 nc.vector.tensor_tensor(
-                    woven_view(parts[u][:, PACK * width :], 2),
-                    rows_view(rows[:, :, u * width : (u + 1) * width], 2),
-                    woven_view(parts[u][:, 0 : PACK * width], 2),
+                    write_order(parts[u][:, PACK * width :], SUB_RUN),
+                    read_order(by_rows(raw[:])[:, :, u * width : (u + 1) * width], SUB_RUN),
+                    write_order(parts[u][:, 0 : PACK * width], SUB_RUN),
                     ALU.subtract,
                 )
 
-            def quant(u, first=0, last=2):
+            def quantize_parts(u, first=0, last=2):
+                cols = slice(width * first, width * last)
                 quantize(
-                    "wx",
                     parts[u][:, PACK * width * first : PACK * width * last],
-                    codes[u][:, width * first : width * last],
-                    scales[u][:, width * first : width * last],
+                    wx_mx[u][0][:, cols],
+                    wx_mx[u][1][:, cols],
                 )
 
-            return trunc, mask, low, quant, codes, scales
+            return truncate, mask, subtract, quantize_parts, wx_mx
 
-        cast_x(0, 0, J // 2, False)
-        s0 = project(0)
-        s1 = project(1)
-        turn(0, s0)
-        turn(1, s1)
-        cast_x(1, 0, J, False)
-        s2 = project(2)
-        turn(2, s2)
-        trunc, mask, low, quant, codes0, scales0 = split_units(0, 256)
-        for step in (trunc, mask, low, quant):
+        weave(x_woven[0][:, 0 : PACK * HALF], x0_raw_left, False)
+        scaled0 = project(0)
+        scaled1 = project(1)
+        turn(0, scaled0)
+        turn(1, scaled1)
+        weave(x_woven[1][:], x1_raw, False)
+        scaled2 = project(2)
+        turn(2, scaled2)
+
+        *steps, wx0_mx = split_steps(0, wx0_raw, HALF)
+        for step in steps:
             step(0)
-        cast_x(0, J // 2, J, True)
+        weave(x_woven[0][:, PACK * HALF :], x0_raw_right, True)
         quantize_x(0)
-        for step in (trunc, mask, low, quant):
+        for step in steps:
             step(1)
-        direct = [2,3]
 
-        ax_banks = [
-            mx_psum.tile([P, N], F32, name="mx_bank%d" % nt) for nt in range(TILES)
-        ]
+        skip_banks = [mx_bank(nt) for nt in range(TILES)]
 
-        def skip_passes(nt, a, codes, scales, width, parts=(0, 1)):
+        def skip_passes(nt, a, wx_mx, width):
             u, c0 = divmod(nt * P, width)
-            for part in parts:
-                ncols = slice(part * width + c0, part * width + c0 + P)
-                if nt in direct:
-                    nc.tensor.matmul_mx(
-                        out=ax_banks[nt][:],
-                        lhsT=codes[u][:, ncols].bitcast(FP8X4),
-                        lhsT_scale=scales[u][:, ncols],
-                        rhs=x_codes[a][:].bitcast(FP8X4),
-                        rhs_scale=x_scales[a][:],
-                        start=(a == 0 and part == 0),
-                        stop=(a == 1 and part == 1),
-                    )
+            for part in range(2):
+                channels = slice(part * width + c0, part * width + c0 + P)
+                first, last = (a, part) == (0, 0), (a, part) == (1, 1)
+                if nt >= TURNED_TILES:
+                    mx_pass(skip_banks[nt][:], wx_mx[u], channels, x_mx[a], slice(0, J), first, last)
                     continue
                 for jt in range(TILES):
-                    jcols = slice(jt * P, (jt + 1) * P)
-                    nc.tensor.matmul_mx(
-                        out=ax_banks[nt][:, jcols],
-                        lhsT=x_codes[a][:, jcols].bitcast(FP8X4),
-                        lhsT_scale=x_scales[a][:, jcols],
-                        rhs=codes[u][:, ncols].bitcast(FP8X4),
-                        rhs_scale=scales[u][:, ncols],
-                        start=(a == 0 and part == 0 and jt == 0),
-                        stop=(a == 1 and part == 1 and jt == TILES - 1),
+                    places = slice(jt * P, (jt + 1) * P)
+                    mx_pass(
+                        skip_banks[nt][:, places], x_mx[a], places, wx_mx[u], channels,
+                        first and jt == 0, last and jt == TILES - 1,
                     )
 
-        trunc, mask, low, quant, codes1, scales1 = split_units(1, P)
+        truncate, mask, subtract, quantize_parts, wx1_mx = split_steps(1, wx1_raw, P)
 
-        def finish(nt):
-            skip_passes(nt, 1, codes1, scales1, P)
+        def finish_turned(nt):
+            skip_passes(nt, 1, wx1_mx, P)
+            skip = sbuf("skip%d" % nt, J, F32)
+            nc.scalar.activation(skip[:], skip_banks[nt][:], ACT.Copy)
+            for jt in range(TILES):
+                add_transposed(nt, jt, skip[:, jt * P : (jt + 1) * P], False, jt == TILES - 1)
             result = sbuf("result%d" % nt, J, F32)
-            if nt in direct:
-                if nt == TILES - 1:
-                    for h in range(2):
-                        cols = slice(h * 256, (h + 1) * 256)
-                        tot = sbuf("tot%d" % h, 256, F32)
-                        res = sbuf("res%d" % h, 256, F32)
-                        nc.vector.tensor_tensor(tot[:], ax_banks[nt][:, cols], interpolated[nt][:, cols], ALU.add)
-                        if h == 0:
-                            nc.scalar.activation(res[:], tot[:], ACT.Relu)
-                            nc.scalar.dma_start(out=out[nt * P : (nt + 1) * P, cols], in_=res[:])
-                        else:
-                            nc.vector.tensor_scalar(res[:], tot[:], 0.0, None, ALU.max)
-                            nc.sync.dma_start(out=out[nt * P : (nt + 1) * P, cols], in_=res[:])
-                    return
-                total = sbuf("total%d" % nt, J, F32)
-                nc.vector.tensor_tensor(total[:], ax_banks[nt][:], interpolated[nt][:], ALU.add)
-                if nt in [3]:
-                    nc.vector.tensor_scalar(result[:], total[:], 0.0, None, ALU.max)
-                else:
-                    nc.scalar.activation(result[:], total[:], ACT.Relu)
-            else:
-                ax = sbuf("ax%d" % nt, J, F32)
-                nc.scalar.activation(ax[:], ax_banks[nt][:], ACT.Copy)
-                for jt in range(TILES):
-                    add_transposed(nt, jt, ax[:, jt * P : (jt + 1) * P], False, jt == TILES - 1)
-                nc.scalar.activation(result[:], out_banks[nt][:], ACT.Relu)
+            nc.scalar.activation(result[:], out_banks[nt][:], ACT.Relu)
             nc.sync.dma_start(out=out[nt * P : (nt + 1) * P, :], in_=result[:])
 
-        skip_passes(0, 0, codes0, scales0, 256)
-        skip_passes(1, 0, codes0, scales0, 256)
+        def finish_direct(nt, interpolated, c0, c1, relu_on_vector, queue, slot=None):
+            total = sbuf("total%d_%d" % (nt, c0), c1 - c0, F32, slot=slot)
+            nc.vector.tensor_tensor(total[:], skip_banks[nt][:, c0:c1], interpolated[:, c0:c1], ALU.add)
+            result = sbuf("result%d_%d" % (nt, c0), c1 - c0, F32)
+            if relu_on_vector:
+                nc.vector.tensor_scalar(result[:], total[:], 0.0, None, ALU.max)
+            else:
+                nc.scalar.activation(result[:], total[:], ACT.Relu)
+            queue.dma_start(out=out[nt * P : (nt + 1) * P, c0:c1], in_=result[:])
+
+        skip_passes(0, 0, wx0_mx, HALF)
+        skip_passes(1, 0, wx0_mx, HALF)
         quantize_x(1)
-        trunc(0)
-        trunc(1, True)
+        truncate(0, 0 in SCALAR_TRUNCATES)
+        truncate(1, 1 in SCALAR_TRUNCATES)
         mask(0)
-        low(0)
+        subtract(0)
         mask(1)
-        quant(0)
-        trunc(2, True)
-        trunc(3, True)
-        finish(0)
-        skip_passes(2, 0, codes0, scales0, 256)
-        skip_passes(3, 0, codes0, scales0, 256)
-        low(1)
+        quantize_parts(0)
+        truncate(2, 2 in SCALAR_TRUNCATES)
+        truncate(3, 3 in SCALAR_TRUNCATES)
+        finish_turned(0)
+        skip_passes(2, 0, wx0_mx, HALF)
+        skip_passes(3, 0, wx0_mx, HALF)
+        subtract(1)
         mask(2)
-        quant(1)
-        finish(1)
+        quantize_parts(1)
+        finish_turned(1)
         interpolated = {}
-        for nt in direct:
+        for nt in range(TURNED_TILES, TILES):
             interpolated[nt] = sbuf("interpolated%d" % nt, J, F32)
             nc.scalar.activation(interpolated[nt][:], out_banks[nt][:], ACT.Copy)
-        low(2)
+        subtract(2)
         mask(3)
-        quant(2)
-        quant(3, 0, 1)
-        low(3)
-        quant(3, 1, 2)
-        finish(2)
-        finish(3)
+        quantize_parts(2)
+        quantize_parts(3, 0, 1)
+        subtract(3)
+        quantize_parts(3, 1, 2)
+        skip_passes(2, 1, wx1_mx, P)
+        finish_direct(2, interpolated[2], 0, J, False, nc.sync)
+        skip_passes(3, 1, wx1_mx, P)
+        finish_direct(3, interpolated[3], 0, HALF, False, nc.scalar)
+        finish_direct(3, interpolated[3], HALF, J, True, nc.sync)

@@ -24,11 +24,11 @@ HALF = J // 2
 LIST_COLS = J // 16
 HI_MASK = 0xFFF0FFF0 - (1 << 32)
 W_HEAD = 256
-COPY_RUN = 4
+COPY_RUN = 2
 SUB_RUN = 2
 TURNED_TILES = 2
 LAST_BANKS = 2
-SCALAR_TRUNCATES = (2, 3)
+SCALAR_TRUNCATES = (1, 2, 3)
 
 
 def by_rows(raw):
@@ -160,10 +160,11 @@ def tile_list_interp_hl_relu_kernel(
             return scaled
 
         def turn(g, scaled):
-            for jt in range(TILES):
+            order = (1, 0, 3, 2)
+            for jt in order:
                 for nt in range(TILES):
-                    first = g == 0 and jt == 0
-                    last = g == G - 1 and jt == TILES - 1 and nt >= TURNED_TILES
+                    first = g == 0 and jt == order[0]
+                    last = g == G - 1 and jt == order[-1] and nt >= TURNED_TILES
                     add_transposed(nt, jt, scaled[:, jt * N + nt * P : jt * N + (nt + 1) * P], first, last)
 
         x_woven = [sbuf("x_woven%d" % a, PACK * J, BF16) for a in range(2)]
@@ -215,10 +216,10 @@ def tile_list_interp_hl_relu_kernel(
         scaled0 = project(0)
         scaled1 = project(1)
         turn(0, scaled0)
-        turn(1, scaled1)
-        weave(x_woven[1][:], x1_raw, False)
         scaled2 = project(2)
+        turn(1, scaled1)
         turn(2, scaled2)
+        weave(x_woven[1][:], x1_raw, False)
 
         *steps, wx0_mx = split_steps(0, wx0_raw, HALF)
         for step in steps:

@@ -24,8 +24,8 @@ HALF = J // 2
 LIST_COLS = J // 16
 HI_MASK = 0xFFF0FFF0 - (1 << 32)
 W_HEAD = 256
-COPY_RUN = 2
-SUB_RUN = 2
+COPY_RUN = 4
+SUB_RUN = 4
 TURNED_TILES = 2
 LAST_BANKS = 2
 SCALAR_TRUNCATES = (1, 2, 3)
@@ -97,10 +97,10 @@ def tile_list_interp_hl_relu_kernel(
 
         w_raw_head = load_rows("w_raw_head", w, 0, 0, W_HEAD)
         nc.sync.dma_start(offsets[:], offs)
-        for q in range(4):
+        for r in range(4):
             nc.sync.dma_start(
-                out=table_scales[32 * q : 32 * q + 4, :].bitcast(I32),
-                in_=tab_scales[0, 4 * q : 4 * q + 4, :].bitcast(I32),
+                out=table_scales[r:P:32, :].bitcast(I32),
+                in_=tab_scales[0, r:16:4, :].bitcast(I32),
             )
         w_raw_rest = load_rows("w_raw_rest", w, 0, W_HEAD, N)
         table_words = sbuf("table_words", T, U32)

from contextlib import ExitStack

import concourse.mybir as mybir
from concourse.masks import make_identity

K, L, N, T, J, G = 512, 1024, 512, 2048, 512, 3
FLOPS = 2 * N * J * (G * K + 2 * L)

F32 = mybir.dt.float32
BF16 = mybir.dt.bfloat16
I32 = mybir.dt.int32
U32 = mybir.dt.uint32
U16 = mybir.dt.uint16
U8 = mybir.dt.uint8
FP8X4 = mybir.dt.float8_e4m3fn_x4
ALU = mybir.AluOpType
ACT = mybir.ActivationFunctionType

P = 128
PACK = 4
K_PASS = P * PACK
TILES = N // P
HALF = J // 2
LIST_COLS = J // 16
HI_MASK = 0xFFF0FFF0 - (1 << 32)
W_HEAD = 256
COPY_RUN = 4
SUB_RUN = 4
TURNED_TILES = 2
LAST_BANKS = 2
SCALAR_TRUNCATES = (1, 2, 3)


def by_rows(raw):
    return raw.rearrange("p (t c) -> p t c", t=PACK)


def read_order(rows, run):
    return rows.rearrange("p t (c i) -> p c t i", i=run)


def write_order(woven, run):
    return woven.rearrange("p (c i t) -> p c t i", i=run, t=PACK)


def tile_list_interp_hl_relu_kernel(
    tc, tab_words, tab_scales, w, x, wx, iw0, iw1, iw2, offs, out
):
    nc = tc.nc
    with ExitStack() as ctx:
        sb = ctx.enter_context(tc.tile_pool(name="sb", bufs=1))
        psum = ctx.enter_context(tc.psum_pool(name="psum", bufs=1))

        def sbuf(name, width, dtype, slot=None):
            return sb.tile([P, width], dtype, name=name, tag=slot or name, align_bytes=64)

        def mx_bank(b):
            return psum.tile([P, N], F32, name="mx_bank%d" % b)

        def load_rows(name, src, a, c0, c1):
            raw = sbuf(name, PACK * (c1 - c0), F32)
            nc.sync.dma_start(
                out=by_rows(raw[:]),
                in_=src[a * K_PASS : (a + 1) * K_PASS, c0:c1].rearrange("(p t) c -> p t c", t=PACK),
            )
            return raw

        def weave(woven, raw, on_vector):
            dst, src = write_order(woven, COPY_RUN), read_order(by_rows(raw[:]), COPY_RUN)
            if on_vector:
                nc.vector.tensor_copy(dst, src)
            else:
                nc.scalar.activation(dst, src, ACT.Copy)

        def quantize(woven, codes, scales):
            nc.vector.quantize_mx(out=codes.bitcast(FP8X4), scales=scales, in_=woven)

        def mx_pass(bank, lhs, lhs_cols, rhs, rhs_cols, start, stop):
            nc.tensor.matmul_mx(
                out=bank,
                lhsT=lhs[0][:, lhs_cols].bitcast(FP8X4),
                lhsT_scale=lhs[1][:, lhs_cols],
                rhs=rhs[0][:, rhs_cols].bitcast(FP8X4),
                rhs_scale=rhs[1][:, rhs_cols],
                start=start,
                stop=stop,
            )

        offsets = sb.tile([P, G * LIST_COLS], U16, name="offsets")
        table_scales = sbuf("table_scales", T, U8)
        nc.vector.memset(table_scales[:, 0 : T // 2].bitcast(I32), 0)
        nc.gpsimd.memset(table_scales[:, T // 2 :].bitcast(I32), 0)
        iw_rows = sbuf("iw_rows", P, F32)
        nc.gpsimd.memset(iw_rows[:], 0.0)
        ident = sbuf("ident", P, F32)
        make_identity(nc, ident[:])

        w_raw_head = load_rows("w_raw_head", w, 0, 0, W_HEAD)
        nc.sync.dma_start(offsets[:], offs)
        for r in range(4):
            nc.sync.dma_start(
                out=table_scales[r:P:32, :].bitcast(I32),
                in_=tab_scales[0, r:16:4, :].bitcast(I32),
            )
        w_raw_rest = load_rows("w_raw_rest", w, 0, W_HEAD, N)
        table_words = sbuf("table_words", T, U32)
        nc.sync.dma_start(
            out=table_words[:].bitcast(I32),
            in_=tab_words[0].rearrange("p t i -> p (t i)").bitcast(I32),
        )
        for g, iw in enumerate((iw0, iw1, iw2)):
            nc.sync.dma_start(
                out=iw_rows[TILES * g : TILES * (g + 1), :], in_=iw.rearrange("(c p) -> c p", p=P)
            )
        x0_raw_left = load_rows("x0_raw_left", x, 0, 0, HALF)
        wx0_raw = load_rows("wx0_raw", wx, 0, 0, N)
        x0_raw_right = load_rows("x0_raw_right", x, 0, HALF, J)
        x1_raw = load_rows("x1_raw", x, 1, 0, J)
        wx1_raw = load_rows("wx1_raw", wx, 1, 0, N)

        picked_scales = sbuf("picked_scales", G * J, U8)
        nc.vector.tensor_copy(picked_scales[:], table_scales[:].indirect(offsets[:]))

        w_woven = sbuf("w_woven", PACK * N, BF16)
        weave(w_woven[:, 0 : PACK * W_HEAD], w_raw_head, False)
        weave(w_woven[:, PACK * W_HEAD :], w_raw_rest, False)
        w_mx = (sbuf("w_codes", N, U32), sbuf("w_scales", N, U8))
        quantize(w_woven[:], w_mx[0][:], w_mx[1][:])

        iw_bank = mx_bank(TILES - 1)
        nc.tensor.transpose(iw_bank[:, 0:P], iw_rows[:], ident[:])
        iw_cols = sbuf("iw_cols", G * TILES, F32)
        nc.scalar.activation(iw_cols[:], iw_bank[:, 0 : G * TILES], ACT.Copy)

        picked_words = sbuf("picked_words", G * J, U32, slot="iw_rows")
        for c0, c1 in ((0, HALF), (HALF, J), (J, 2 * J), (2 * J, 3 * J)):
            nc.vector.tensor_copy(
                picked_words[:, c0:c1], table_words[:].indirect(offsets[:, c0 // 16 : c1 // 16])
            )
        picked_mx = (picked_words, picked_scales)

        out_banks = [psum.tile([P, J], F32, name="out_bank%d" % nt) for nt in range(TILES)]

        def add_transposed(nt, jt, src, start, stop):
            nc.tensor.matmul(
                out_banks[nt][:, jt * P : (jt + 1) * P], src, ident[:],
                is_transpose=True, start=start, stop=stop,
            )

        def project(g):
            scaled = sbuf("scaled%d" % g, TILES * N, F32, slot="x0_raw_left" if g == 0 else None)
            for jt in range(TILES):
                bank = mx_bank(jt if g < G - 1 else TILES - LAST_BANKS + jt % LAST_BANKS)
                places = slice(g * J + jt * P, g * J + (jt + 1) * P)
                mx_pass(bank[:], picked_mx, places, w_mx, slice(0, N), True, True)
                col = TILES * g + jt
                nc.scalar.activation(
                    scaled[:, jt * N : (jt + 1) * N], bank[:], ACT.Copy, scale=iw_cols[:, col : col + 1]
                )
            return scaled

        def turn(g, scaled):
            order = (1, 0, 3, 2)
            for jt in order:
                for nt in range(TILES):
                    first = g == 0 and jt == order[0]
                    last = g == G - 1 and jt == order[-1] and nt >= TURNED_TILES
                    add_transposed(nt, jt, scaled[:, jt * N + nt * P : jt * N + (nt + 1) * P], first, last)

        x_woven = [sbuf("x_woven%d" % a, PACK * J, BF16) for a in range(2)]
        x_mx = [(sbuf("x_codes%d" % a, J, U32), sbuf("x_scales%d" % a, J, U8)) for a in range(2)]

        def quantize_x(a):
            quantize(x_woven[a][:], x_mx[a][0][:], x_mx[a][1][:])

        def split_steps(a, raw, width):
            count = N // width
            parts = [sbuf("parts%d_%d" % (a, u), 2 * PACK * width, BF16) for u in range(count)]
            wx_mx = [
                (sbuf("wx_codes%d_%d" % (a, u), 2 * width, U32), sbuf("wx_scales%d_%d" % (a, u), 2 * width, U8))
                for u in range(count)
            ]
            upper_halves = raw[:].bitcast(BF16).rearrange("p (t c h) -> p t c h", t=PACK, h=2)

            def truncate(u, on_scalar=False):
                dst = write_order(parts[u][:, 0 : PACK * width], COPY_RUN)
                src = read_order(upper_halves[:, :, u * width : (u + 1) * width, 1], COPY_RUN)
                if on_scalar:
                    nc.scalar.copy(dst, src)
                else:
                    nc.vector.tensor_copy(dst, src)

            def mask(u):
                hi_pairs = parts[u][:, 0 : PACK * width].bitcast(I32)
                nc.vector.tensor_scalar(hi_pairs, hi_pairs, HI_MASK, None, ALU.bitwise_and)

            def subtract(u):
                nc.vector.tensor_tensor(
                    write_order(parts[u][:, PACK * width :], SUB_RUN),
                    read_order(by_rows(raw[:])[:, :, u * width : (u + 1) * width], SUB_RUN),
                    write_order(parts[u][:, 0 : PACK * width], SUB_RUN),
                    ALU.subtract,
                )

            def quantize_parts(u, first=0, last=2):
                cols = slice(width * first, width * last)
                quantize(
                    parts[u][:, PACK * width * first : PACK * width * last],
                    wx_mx[u][0][:, cols],
                    wx_mx[u][1][:, cols],
                )

            return truncate, mask, subtract, quantize_parts, wx_mx

        weave(x_woven[0][:, 0 : PACK * HALF], x0_raw_left, False)
        scaled0 = project(0)
        scaled1 = project(1)
        turn(0, scaled0)
        scaled2 = project(2)
        turn(1, scaled1)
        turn(2, scaled2)
        weave(x_woven[1][:], x1_raw, False)

        *steps, wx0_mx = split_steps(0, wx0_raw, HALF)
        for step in steps:
            step(0)
        weave(x_woven[0][:, PACK * HALF :], x0_raw_right, True)
        quantize_x(0)
        for step in steps:
            step(1)

        skip_banks = [mx_bank(nt) for nt in range(TILES)]

        def skip_passes(nt, a, wx_mx, width):
            u, c0 = divmod(nt * P, width)
            for part in range(2):
                channels = slice(part * width + c0, part * width + c0 + P)
                first, last = (a, part) == (0, 0), (a, part) == (1, 1)
                if nt >= TURNED_TILES:
                    mx_pass(skip_banks[nt][:], wx_mx[u], channels, x_mx[a], slice(0, J), first, last)
                    continue
                for jt in range(TILES):
                    places = slice(jt * P, (jt + 1) * P)
                    mx_pass(
                        skip_banks[nt][:, places], x_mx[a], places, wx_mx[u], channels,
                        first and jt == 0, last and jt == TILES - 1,
                    )

        truncate, mask, subtract, quantize_parts, wx1_mx = split_steps(1, wx1_raw, P)

        def finish_turned(nt):
            skip_passes(nt, 1, wx1_mx, P)
            skip = sbuf("skip%d" % nt, J, F32)
            nc.scalar.activation(skip[:], skip_banks[nt][:], ACT.Copy)
            for jt in range(TILES):
                add_transposed(nt, jt, skip[:, jt * P : (jt + 1) * P], False, jt == TILES - 1)
            result = sbuf("result%d" % nt, J, F32)
            nc.scalar.activation(result[:], out_banks[nt][:], ACT.Relu)
            nc.sync.dma_start(out=out[nt * P : (nt + 1) * P, :], in_=result[:])

        def finish_direct(nt, interpolated, c0, c1, relu_on_vector, queue, slot=None):
            total = sbuf("total%d_%d" % (nt, c0), c1 - c0, F32, slot=slot)
            nc.vector.tensor_tensor(total[:], skip_banks[nt][:, c0:c1], interpolated[:, c0:c1], ALU.add)
            result = sbuf("result%d_%d" % (nt, c0), c1 - c0, F32)
            if relu_on_vector:
                nc.vector.tensor_scalar(result[:], total[:], 0.0, None, ALU.max)
            else:
                nc.scalar.activation(result[:], total[:], ACT.Relu)
            queue.dma_start(out=out[nt * P : (nt + 1) * P, c0:c1], in_=result[:])

        skip_passes(0, 0, wx0_mx, HALF)
        skip_passes(1, 0, wx0_mx, HALF)
        quantize_x(1)
        truncate(0, 0 in SCALAR_TRUNCATES)
        truncate(1, 1 in SCALAR_TRUNCATES)
        mask(0)
        subtract(0)
        mask(1)
        quantize_parts(0)
        truncate(2, 2 in SCALAR_TRUNCATES)
        truncate(3, 3 in SCALAR_TRUNCATES)
        finish_turned(0)
        skip_passes(2, 0, wx0_mx, HALF)
        skip_passes(3, 0, wx0_mx, HALF)
        subtract(1)
        mask(2)
        quantize_parts(1)
        finish_turned(1)
        interpolated = {}
        for nt in range(TURNED_TILES, TILES):
            interpolated[nt] = sbuf("interpolated%d" % nt, J, F32)
            nc.scalar.activation(interpolated[nt][:], out_banks[nt][:], ACT.Copy)
        subtract(2)
        mask(3)
        quantize_parts(2)
        quantize_parts(3, 0, 1)
        subtract(3)
        quantize_parts(3, 1, 2)
        skip_passes(2, 1, wx1_mx, P)
        finish_direct(2, interpolated[2], 0, J, False, nc.sync)
        skip_passes(3, 1, wx1_mx, P)
        finish_direct(3, interpolated[3], 0, HALF, False, nc.scalar)
        finish_direct(3, interpolated[3], HALF, J, True, nc.sync)
